import numpy as np
import ml_dtypes


def mxq(x, axis, fmt="e4m3"):
    dtype, down = {"e4m3": (ml_dtypes.float8_e4m3fn, 7), "e5m2": (ml_dtypes.float8_e5m2, 14)}[fmt]
    v = np.moveaxis(np.asarray(x, np.float32).astype(ml_dtypes.bfloat16).astype(np.float64), axis, -1)
    blocks = v.reshape(v.shape[:-1] + (-1, 32))
    amax = np.abs(blocks).max(-1, keepdims=True)
    byte = np.maximum(np.where(amax > 0, np.frexp(amax)[1] - 1 + 127, 0) - down, 1)
    scale = np.exp2(byte - 127.0)
    codes = (blocks / scale).astype(np.float32).astype(dtype).astype(np.float64)
    return np.moveaxis((codes * scale).reshape(v.shape), -1, axis)


WIDE = False


def mx_kscale(k):
    if not WIDE:
        return np.ones(k)
    levels = np.array([10, -10, 5, -5, 0])
    if k % 512:
        return np.exp2(np.random.permutation(np.resize(levels, k // 32))).repeat(32)
    a = np.empty((k // 512, 16))
    for p in range(k // 512):
        a[p, :8] = np.random.permutation(np.resize(levels, 8))
        for g in range(8):
            far = levels[np.abs(levels - a[p, g]) >= 10]
            a[p, g + 8] = far[np.random.randint(len(far))]
    return np.exp2(a.ravel()).repeat(32)


def f64(x):
    return np.asarray(x).astype(np.float64)


def striped(idx):
    return np.tile(idx.reshape(-1, 16).T, (8, 1)).astype(np.uint16)


def unstriped(offs):
    return offs[:16].T.reshape(-1).astype(np.int64)


def pack_weight(w):
    k, n = w.shape
    w = f64(np.asarray(w, np.float32).astype(ml_dtypes.bfloat16)).reshape(k // 32, 32, n)
    amax = np.abs(w).max(1)
    byte = np.clip(np.where(amax > 0, np.frexp(amax)[1] - 1 + 127 - 7, 1), 1, 254)
    scaled = (w * np.exp2(127.0 - byte)[:, None, :]).reshape(k, n).astype(np.float32)
    words = np.ascontiguousarray(scaled.reshape(k // 512, 128, 4, n).transpose(0, 1, 3, 2)).astype(ml_dtypes.float8_e4m3fn).view(np.uint8)
    return words, np.ascontiguousarray(byte.astype(np.uint8).reshape(k // 512, 16, n))


def unpack_weight(words, scales):
    g, p, n, _ = words.shape
    vals = np.ascontiguousarray(words).view(ml_dtypes.float8_e4m3fn).astype(np.float64) * np.repeat(np.exp2(scales.astype(np.float64) - 127.0), 8, axis=1)[..., None]
    return vals.transpose(0, 1, 3, 2).reshape(g * 512, n)


E2M1 = np.array([0.0, 0.5, 1.0, 1.5, 2.0, 3.0, 4.0, 6.0, -0.0, -0.5, -1.0, -1.5, -2.0, -3.0, -4.0, -6.0])


def pack_fp4(w):
    k, n = w.shape
    w = f64(np.asarray(w, np.float32).astype(ml_dtypes.bfloat16)).reshape(k // 32, 32, n)
    amax = np.abs(w).max(1)
    mant, ex = np.frexp(amax / 6.0)
    byte = np.clip(np.where(amax > 0, np.where(mant > 0.5, ex, ex - 1) + 127, 1), 1, 254)
    scaled = (w * np.exp2(127.0 - byte)[:, None, :]).reshape(k, n).astype(np.float32)
    c = np.ascontiguousarray(scaled.reshape(k // 512, 128, 4, n).transpose(0, 1, 3, 2)).astype(ml_dtypes.float4_e2m1fn).view(np.uint8) & 0xF
    words = (c[..., 0::2] | (c[..., 1::2] << 4)).reshape(k // 512, 128, 2 * n)
    return np.ascontiguousarray(words), np.ascontiguousarray(byte.astype(np.uint8).reshape(k // 512, 16, n))


def unpack_fp4(words, scales):
    g, _, n = scales.shape
    words = np.ascontiguousarray(words).reshape(g, 128, n, 2)
    nib = np.empty((g, 128, n, 4), np.uint8)
    nib[..., 0::2] = words & 0xF
    nib[..., 1::2] = words >> 4
    vals = E2M1[nib] * np.repeat(np.exp2(scales.astype(np.float64) - 127.0), 8, axis=1)[..., None]
    return vals.transpose(0, 1, 3, 2).reshape(g * 512, n)


def planes(y):
    n, m = y.shape
    v = y.astype(np.float32).astype(ml_dtypes.bfloat16).astype(np.float64).reshape(n // 32, 32, m)
    top = np.abs(v).max(1)
    byte = np.clip(np.where(top > 0, np.frexp(top)[1] - 1 + 127 - 7, 1), 1, 254)
    codes = (v * np.exp2(127.0 - byte)[:, None, :]).reshape(n, m).astype(np.float32).astype(ml_dtypes.float8_e4m3fn).view(np.uint8)
    words = codes.reshape(n // 512, 128, 4, m).transpose(0, 1, 3, 2)
    return np.ascontiguousarray(words), np.ascontiguousarray(byte.astype(np.uint8).reshape(n // 512, 16, m))


K, T, S, N, H = 512, 1024, 512, 512, 512


def setup_inputs():
    n = np.random.standard_normal
    s = mx_kscale(K)[:, None]
    u = mx_kscale(H)
    packed_xT = pack_weight(n((K, T)) * s)
    packed_w1 = pack_fp4(n((K, N)) / np.sqrt(K) / s)
    packed_w2 = pack_fp4(n((K, N)) / np.sqrt(K) / s)
    packed_w3 = pack_fp4(n((H, N)) / np.sqrt(H) / u[:, None])
    return {
        "x_words": packed_xT[0],
        "x_scales": packed_xT[1],
        "w1_words": packed_w1[0],
        "w1_scales": packed_w1[1],
        "w2_words": packed_w2[0],
        "w2_scales": packed_w2[1],
        "twr": (np.random.uniform(-1.0, 1.0, (H, S))).astype(np.float32),
        "twi": (np.random.uniform(-1.0, 1.0, (H, S))).astype(np.float32),
        "unit": (np.random.uniform(0.6, 1.4, (H, 1)) * u[:, None]).astype(np.float32),
        "w3_words": packed_w3[0],
        "w3_scales": packed_w3[1],
        "offs": striped(np.random.permutation(T)[:S]),
        "b1": striped(np.random.permutation(S)),
        "b2": striped(np.random.permutation(S)),
    }


def reference(x_words, x_scales, w1_words, w1_scales, w2_words, w2_scales, twr, twi, unit, w3_words, w3_scales, offs, b1, b2):
    xq = unpack_weight(x_words, x_scales)[:, unstriped(offs)]
    re = unpack_fp4(w1_words, w1_scales).T @ xq
    pr = re[:, unstriped(b1)]
    im2 = unpack_fp4(w2_words, w2_scales).T @ xq
    pi1 = im2[:, unstriped(b1)]
    xr = re + f64(twr) * pr - (f64(twi) * pi1)
    xp = xr[:, unstriped(b2)]
    yr1 = xr - xp
    xi = im2 + f64(twr) * pi1 + f64(twi) * pr
    xq = xi[:, unstriped(b2)]
    yi1 = xi + xq
    hid = f64(unit) * (yr1 * yi1 + xr)
    out_0 = unpack_fp4(w3_words, w3_scales).T @ mxq(hid, 0, "e4m3")
    return (out_0,) + planes(out_0)

from contextlib import ExitStack

import concourse.mybir as mybir
from concourse.masks import make_identity

K, T, S, N, H = 512, 1024, 512, 512, 512
FLOPS = 3 * 2 * 512 * 512 * 512

F32 = mybir.dt.float32
BF16 = mybir.dt.bfloat16
I32 = mybir.dt.int32
U32 = mybir.dt.uint32
U16 = mybir.dt.uint16
U8 = mybir.dt.uint8
FP8X4 = mybir.dt.float8_e4m3fn_x4
FP4X4 = mybir.dt.float4_e2m1fn_x4
MULT = mybir.AluOpType.mult
ADD = mybir.AluOpType.add
SUB = mybir.AluOpType.subtract
COPY = mybir.ActivationFunctionType.Copy

P = 128
ROW_TILES = H // P
SPARE = 8
HALF = S // 2


def tile_picked_ybutfly_mul_po_kernel(
    tc, x_words, x_scales, w1_words, w1_scales, w2_words, w2_scales, twr, twi, unit,
    w3_words, w3_scales, offs, b1, b2, out_0, out_1, out_2,
):
    nc = tc.nc
    with ExitStack() as ctx:
        keep = ctx.enter_context(tc.tile_pool(name="keep", bufs=1))
        work = ctx.enter_context(tc.tile_pool(name="work", bufs=2))
        psum = ctx.enter_context(tc.psum_pool(name="psum", bufs=1))

        def load_scale_rows(queue, plane, scales):
            for q in range(4):
                queue.dma_start(out=plane[32 * q : 32 * q + 4, :].bitcast(I32), in_=scales[0, 4 * q : 4 * q + 4, :].bitcast(I32))

        def offsets(list_tile, lo, hi):
            return list_tile[:, lo // 16 : hi // 16]

        xs_all = keep.tile([P, T], U8, name="xs_all", align_bytes=64)
        w1s = keep.tile([P, N], U8, name="w1s", align_bytes=64)
        w2s = keep.tile([P, N], U8, name="w2s", align_bytes=64)
        w3s_raw = keep.tile([P, N], U8, name="w3s_raw", align_bytes=64)
        for plane in (xs_all, w1s, w2s, w3s_raw):
            nc.vector.memset(plane[:].bitcast(I32), 0)

        xw_all = keep.tile([P, T], I32, name="xw_all", align_bytes=64)
        load_scale_rows(nc.sync, xs_all, x_scales)
        offs_sb = keep.tile([P, S // 16], U16, name="offs_sb")
        nc.sync.dma_start(offs_sb[:], offs)
        w1w = keep.tile([P, 2 * N], U8, name="w1w", align_bytes=64)
        nc.sync.dma_start(out=w1w[:].bitcast(I32), in_=w1_words[0].bitcast(I32))
        w2w = keep.tile([P, 2 * N], U8, name="w2w", align_bytes=64)
        nc.sync.dma_start(out=w2w[:].bitcast(I32), in_=w2_words[0].bitcast(I32))
        nc.sync.dma_start(out=xw_all[:], in_=x_words[0].rearrange("p c r -> p (c r)").bitcast(I32))
        load_scale_rows(nc.sync, w1s, w1_scales)
        load_scale_rows(nc.sync, w2s, w2_scales)
        b1_sb = keep.tile([P, S // 16], U16, name="b1_sb")
        nc.sync.dma_start(b1_sb[:], b1)
        w3w_raw = keep.tile([P, 2 * N], U8, name="w3w_raw", align_bytes=64)
        nc.gpsimd.dma_start(out=w3w_raw[:].bitcast(I32), in_=w3_words[0].bitcast(I32))

        twr_sb, twi_sb = [], []
        unit_sb = keep.tile([P, ROW_TILES], F32, name="unit_sb")
        b2_sb = keep.tile([P, S // 16], U16, name="b2_sb")
        for a in range(ROW_TILES):
            rows = slice(a * P, (a + 1) * P)
            twr_sb.append(keep.tile([P, S], F32, name="twr%d" % a))
            twi_sb.append(keep.tile([P, S], F32, name="twi%d" % a))
            nc.sync.dma_start(out=twr_sb[a][:], in_=twr[rows, :])
            if a == 0:
                with nc.allow_non_contiguous_dma(reason="one factor a row, four rows a partition"):
                    nc.sync.dma_start(out=unit_sb[:], in_=unit.rearrange("(a p) o -> p (a o)", p=P))
            nc.sync.dma_start(out=twi_sb[a][:], in_=twi[rows, :])
            if a == 0:
                nc.sync.dma_start(b2_sb[:], b2)

        load_scale_rows(nc.sync, w3s_raw, w3_scales)
        windows = {}
        for a in range(ROW_TILES):
            for kind in ("re", "im", "xr", "xi"):
                windows[kind, a] = keep.tile([P, S + SPARE], F32, name="%s%d" % (kind, a))
                nc.vector.memset(windows[kind, a][:, S:], 0.0)
        ident = keep.tile([P, P], F32, name="ident")
        make_identity(nc, ident[:])

        xs = keep.tile([P, S], U8, name="xs", align_bytes=64)
        xw = keep.tile([P, S], U32, name="xw", align_bytes=64)
        nc.vector.tensor_copy(xs[:], xs_all[:].indirect(offs_sb[:]))
        nc.vector.tensor_copy(xw[:], xw_all[:].bitcast(U32).indirect(offs_sb[:]))

        w3w = keep.tile([P, 2 * N], U8, name="w3w", align_bytes=64)
        w3s = keep.tile([P, N], U8, name="w3s", align_bytes=64)
        nc.scalar.copy(out=w3w[:].bitcast(U16).rearrange("p (t m) -> p t m", t=4), in_=w3w_raw[:].bitcast(U16).rearrange("p (m t) -> p t m", t=4))

        pieces = ((0, 2), (2, 1), (3, 1))
        hid_t = {first: keep.tile([P, count, H], BF16, name="hid_t%d" % first, align_bytes=64) for first, count in pieces}
        y_scales = keep.tile([P, S], U8, name="y_scales", align_bytes=64)
        partner, sums, turned = {}, {}, {}

        def new_bank(shape, name):
            return psum.tile(shape, F32, name=name, tag="bank", bufs=8)

        def first_products(a):
            for kind, words, plane in (("re", w1w, w1s), ("im", w2w, w2s)):
                bank = new_bank([P, S], "first")
                nc.tensor.matmul_mx(
                    out=bank[:], lhsT=words[:, 2 * P * a : 2 * P * (a + 1)].bitcast(FP4X4), lhsT_scale=plane[:, P * a : P * (a + 1)],
                    rhs=xw[:].bitcast(FP8X4), rhs_scale=xs[:], start=True, stop=True)
                window = windows[kind, a]
                got = keep.tile([P, S], F32, name="p_%s%d" % (kind, a))
                partner[kind, a] = got
                if a == 0 and kind == "im":
                    nc.vector.tensor_copy(out=window[:, :S], in_=bank[:])
                    for lo in (0, HALF):
                        nc.vector.tensor_copy(got[:, lo : lo + HALF], window[:].indirect(offsets(b1_sb, lo, lo + HALF)))
                else:
                    nc.scalar.copy(out=window[:, :S], in_=bank[:])
                    nc.scalar.activation(got[:], window[:].indirect(b1_sb[:]), COPY)

        def rotate(a):
            u = unit_sb[:, a : a + 1]
            pr, pi = partner["re", a], partner["im", a]
            rr = work.tile([P, S], F32, name="rr")
            ir = work.tile([P, S], F32, name="ir")
            ii = work.tile([P, S], F32, name="ii")
            ri = work.tile([P, S], F32, name="ri")
            sr = work.tile([P, S], F32, name="sr")
            si = keep.tile([P, S], F32, name="si%d" % a)
            sums[a] = si
            steps = {
                "rr": lambda: nc.vector.scalar_tensor_tensor(out=rr[:], in0=pr[:], scalar=u, in1=twr_sb[a][:], op0=MULT, op1=MULT),
                "ir": lambda: nc.vector.tensor_tensor(out=ir[:], in0=pr[:], in1=twi_sb[a][:], op=MULT),
                "sr": lambda: nc.vector.scalar_tensor_tensor(out=sr[:], in0=windows["re", a][:, :S], scalar=u, in1=rr[:], op0=MULT, op1=ADD),
                "si": lambda: nc.vector.tensor_tensor(out=si[:], in0=windows["im", a][:, :S], in1=ir[:], op=ADD),
                "ii": lambda: nc.vector.scalar_tensor_tensor(out=ii[:], in0=pi[:], scalar=u, in1=twi_sb[a][:], op0=MULT, op1=MULT),
                "ri": lambda: nc.vector.tensor_tensor(out=ri[:], in0=pi[:], in1=twr_sb[a][:], op=MULT),
                "xr": lambda: nc.vector.tensor_tensor(out=windows["xr", a][:, :S], in0=sr[:], in1=ii[:], op=SUB),
                "xi": lambda: nc.vector.tensor_tensor(out=windows["xi", a][:, :S], in0=si[:], in1=ri[:], op=ADD),
            }
            order = "rr ii sr ir xr ri si xi" if a == ROW_TILES - 1 else "rr ir sr si ii ri xr xi"
            for step in order.split():
                steps[step]()

        def fetch_partners(a, first, count):
            lo, hi = first * P, (first + count) * P
            minus_xp = keep.tile([P, count * P], F32, name="minus_xp%d_%d" % (a, first))
            xq = keep.tile([P, count * P], F32, name="xq%d_%d" % (a, first))
            nc.scalar.activation(minus_xp[:], windows["xr", a][:].indirect(offsets(b2_sb, lo, hi)), COPY, scale=-1.0)
            nc.scalar.activation(xq[:], windows["xi", a][:].indirect(offsets(b2_sb, lo, hi)), COPY)
            partner["xr", a, first], partner["xi", a, first] = minus_xp, xq

        def turn(name, count, terms):
            bank = new_bank([P, 4, P], name)
            passes = [(term, col, b) for term, col in terms for b in range(count)]
            for n, (term, col, b) in enumerate(passes):
                nc.tensor.matmul(out=bank[:, b, :], lhsT=term[:, col + b * P : col + (b + 1) * P], rhs=ident[:], is_transpose=True,
                                 start=(n == 0), stop=(n == len(passes) - 1))
            return bank

        def turn_sums(a, first, count):
            xr, xi, lo = windows["xr", a], windows["xi", a], first * P
            xr_t = turn("xr_t", count, ((xr, lo),))
            yr_t = turn("yr_t", count, ((xr, lo), (partner["xr", a, first], 0)))
            yi_t = turn("yi_t", count, ((xi, lo), (partner["xi", a, first], 0)))
            turned[a, first] = xr_t, yr_t, yi_t

        def empty_yi(a, first, count, into):
            yi_sb = into[:, : count * P].rearrange("p (b i) -> p b i", i=P)
            nc.scalar.copy(out=yi_sb, in_=turned[a, first][2][:, :count, :])
            turned[a, first] = turned[a, first][:2] + (yi_sb,)

        def combine(a, first, count):
            xr_t, yr_t, yi_sb = turned[a, first]
            prod = work.tile([P, 4, P], F32, name="prod")
            nc.vector.tensor_tensor(out=prod[:, :count, :], in0=yr_t[:, :count, :], in1=yi_sb, op=MULT)
            for start, width in pieces:
                if first <= start < first + count:
                    part = slice(start - first, start - first + width)
                    nc.vector.tensor_tensor(out=hid_t[start][:, :, a * P : (a + 1) * P], in0=xr_t[:, part, :], in1=prod[:, part, :], op=ADD)

        quantised = {}

        def quantise_hid(first, count):
            pairs = new_bank([P, 2, 2, P], "pairs")
            for b in range(count):
                words = hid_t[first][:, b, :].bitcast(F32)
                for u in range(2):
                    nc.tensor.transpose(pairs[:, b, u, :], words[:, u : 2 * P : 2], ident[:])
            hid = keep.tile([P, 4 * count * P], BF16, name="hid%d" % first, align_bytes=64)
            nc.scalar.copy(out=hid[:].bitcast(F32).rearrange("p (b j u) -> p b j u", b=count, u=2),
                           in_=pairs[:, :count].rearrange("p b u j -> p b j u"))
            codes = keep.tile([P, count * P], U32, name="hid_codes%d" % first, align_bytes=64)
            scales = keep.tile([P, count * P], U8, name="hid_scales%d" % first, align_bytes=64)
            nc.vector.quantize_mx(out=codes[:].bitcast(FP8X4), scales=scales[:], in_=hid[:])
            quantised[first] = codes, scales

        def last_product(first, count):
            width = count * P
            cols = slice(first * P, first * P + width)
            codes, scales = quantised[first]
            y = keep.tile([P, 4, width], F32, name="y%d" % first)
            per_bank = 4 // count
            for t0 in range(0, 4, per_bank):
                bank = new_bank([P, per_bank, width], "last")
                for t in range(t0, t0 + per_bank):
                    nc.tensor.matmul_mx(
                        out=bank[:, t - t0, :], lhsT=w3w[:, 2 * P * t : 2 * P * (t + 1)].bitcast(FP4X4), lhsT_scale=w3s[:, P * t : P * (t + 1)],
                        rhs=codes[:].bitcast(FP8X4), rhs_scale=scales[:], start=True, stop=True)
                nc.scalar.copy(out=y[:, t0 : t0 + per_bank, :], in_=bank[:])
            nc.sync.dma_start(out=out_0.rearrange("(p t) j -> p t j", t=4)[:, :, cols], in_=y[:])
            y_round = keep.tile([P, width, 4], BF16, name="y_round%d" % first, align_bytes=64)
            nc.vector.tensor_copy(out=y_round[:], in_=y[:].rearrange("p t j -> p j t"))
            y_codes = keep.tile([P, width], U32, name="y_codes%d" % first, align_bytes=64)
            nc.vector.quantize_mx(out=y_codes[:].bitcast(FP8X4), scales=y_scales[:, cols], in_=y_round[:].rearrange("p j t -> p (j t)"))
            nc.sync.dma_start(out=out_1[0].rearrange("p c r -> p (c r)").bitcast(I32)[:, cols], in_=y_codes[:].bitcast(I32))

        for a in range(ROW_TILES):
            first_products(a)
        rotate(0)
        for a in range(ROW_TILES - 1):
            rotate(a + 1)
            fetch_partners(a, 0, 4)
            turn_sums(a, 0, 4)
            if a > 0:
                empty_yi(a - 1, 0, 4, sums[a])
        last = ROW_TILES - 1
        for first in (0, 2):
            fetch_partners(last, first, 2)
        empty_yi(last - 1, 0, 4, sums[last])
        nc.vector.tensor_copy(out=w3s[:].rearrange("p (t m) -> p t m", t=4), in_=w3s_raw[:].rearrange("p (m t) -> p t m", t=4))
        for a in range(ROW_TILES - 1):
            combine(a, 0, 4)
        for first in (0, 2):
            turn_sums(last, first, 2)
            empty_yi(last, first, 2, keep.tile([P, 2 * P], F32, name="yi_last%d" % first))
            combine(last, first, 2)
        for n, piece in enumerate(pieces):
            quantise_hid(*piece)
            if n > 0:
                last_product(*pieces[n - 1])
        last_product(*pieces[-1])
        for q in range(4):
            queue = nc.sync if q < 2 else nc.scalar
            queue.dma_start(out=out_2[0, 4 * q : 4 * q + 4, :].bitcast(I32), in_=y_scales[32 * q : 32 * q + 4, :].bitcast(I32))
